import numpy as np, ml_dtypes
CORES = [4,20,36,44,92,100,108,116,3,19,35,43,91,99,107,115]
N = 16
T, CAP = 2048, 512
def entries(a): return a.T.reshape(-1)
def pack(v, P): return np.ascontiguousarray(np.asarray(v, np.int32).reshape(-1, P).T)
def lists(rng, how):
    n = rng.integers(0, CAP + 1, (N, 8))
    if how in ("comb", "full"): n[:] = CAP
    if how == "one": n[:] = 1
    if how == "none": n[int(rng.integers(N))] = 0; n[:, int(rng.integers(8))] = 0
    F = np.zeros((N, 8, T), np.int64)
    for r in range(N):
        for h in range(8):
            o = (rng.permutation(16)[:, None] + 16 * np.arange(T // 16)).reshape(-1) if how == "comb" else rng.permutation(T)
            F[r, h, o[:n[r, h]]] = 1
    if how == "run":
        p = rng.permutation(8); n[:, p[:2]] = CAP; n[:, p[2]] = CAP * rng.permutation(np.arange(N) % 2); n[:, p[3]] = 0
        s = rng.integers(0, T - n + 1); s[:, p[0]] = 0; s[:, p[1]] = T - CAP; s[:, p[2]] = 16 * rng.integers(0, max(1, (T - CAP) // 16), N) + 1
        F = ((np.arange(T) >= s[:, :, None]) & (np.arange(T) < (s + n)[:, :, None])).astype(np.int64)
    return {"keep": np.stack([np.concatenate([pack(F[r, h], 16) for h in range(8)], axis=0) for r in range(N)])}
def setup_inputs(rng):
    return dict({"x": rng.standard_normal((N, 128, T), dtype=np.float32).astype(ml_dtypes.bfloat16)}, **lists(rng, "uniform"))
def setup_inputs_comb(rng):
    d = setup_inputs(rng); d.update(lists(rng, "comb"))
    for k in ("x",): d[k] = (d[k].astype(np.float32) * 1048576.0).astype(d[k].dtype)
    return d
def setup_inputs_full(rng):
    d = setup_inputs(rng); d.update(lists(rng, "full"))
    for k in ("x",): d[k] = (d[k].astype(np.float32) * (1 / 1024.0)).astype(d[k].dtype)
    return d
def setup_inputs_none(rng):
    d = setup_inputs(rng); d.update(lists(rng, "none"))
    return d
def setup_inputs_one(rng):
    d = setup_inputs(rng); d.update(lists(rng, "one"))
    return d
def setup_inputs_run(rng):
    d = setup_inputs(rng); d.update(lists(rng, "run"))
    return d
def check_inputs(x):
    bad = []
    if x["keep"].min() < 0 or x["keep"].max() >= 2: bad.append("keep out of range")
    if max(int(a[16 * h:16 * h + 16].sum()) for a in x["keep"] for h in range(8)) > CAP: bad.append("a head keeps more than CAP columns on a rank")
    return bad
def reference(x, keep):
    y = np.zeros((128, N * CAP), x.dtype)
    for h in range(8):
        H = slice(16 * h, 16 * h + 16); got = np.concatenate([x[r][H][:, entries(keep[r][H]) > 0] for r in range(N)], axis=1); y[H, :got.shape[1]] = got
    return {"y": np.broadcast_to(y, (N, 128, N * CAP))}

@@ -1,0 +1,273 @@
+from concourse.bass import DstId, RemoteDMATransfer
+from concourse.mybir import AluOpType, AxisListType, ActivationFunctionType
+
+N, CAP, T_COLS = 16, 512, 2048
+WIDE = N * CAP
+ZERO = WIDE
+WIN = 2688
+
+
+def _s(cols, kind):
+    return ("sbuf", [128, cols], kind)
+
+
+SCRATCH = {"psa": ("psum", [128, 512], "float32"), "psb": ("psum", [128, 512], "float32"),
+           "psc": ("psum", [128, 512], "float32"),
+           "kp": _s(128, "int32"), "pint": _s(2, "int32"), "pdi": _s(2, "int32"), "bli": _s(4, "int32"),
+           "offu": _s(128, "uint16"), "offs": _s(512, "uint16"),
+           "xs": _s(T_COLS, "bfloat16"), "win": _s(WIN, "bfloat16"), "land": _s(WIDE + 16, "bfloat16"),
+           "yo": _s(WIDE, "bfloat16"), "ga": _s(512, "bfloat16"), "gb": _s(512, "bfloat16")}
+for _n in ("kb", "nk", "ones", "half", "blk", "tri", "irow", "ia", "imge", "imlt", "la", "lb", "lc", "ld"):
+    SCRATCH[_n] = _s(128, "bfloat16")
+for _n in ("nkt", "tgrid", "cinc", "qf", "off"):
+    SCRATCH[_n] = _s(128, "float32")
+for _n in ("cnt", "rr", "mle", "meq", "m1", "m2"):
+    SCRATCH[_n] = _s(N, "float32")
+for _n in ("g16", "qg", "srcf"):
+    SCRATCH[_n] = _s(512, "float32")
+for _n in ("imod", "pcol", "nn", "pd", "blf"):
+    SCRATCH[_n] = _s(4, "float32")
+
+PIECES = [("v", 4096, 1024), ("s", 6144, 1024), ("v", 5120, 1024), ("s", 7168, 1024),
+          ("v", 0, 1024), ("s", 2048, 1024), ("v", 1024, 1024), ("s", 3072, 1024)]
+SEMAPHORES = (["ldk", "ldx", "vv", "gk", "pe1", "pe2", "pe3", "cin", "loc", "ys"]
+              + ["b%d" % r for r in range(N)] + ["p%d" % k for k in range(len(PIECES))])
+_cache = {}
+
+
+def roles(cores, topo):
+    everyone = range(128)
+    on_chip = {}
+    for c in everyone:
+        on_chip.setdefault(topo.chip(c), []).append(c)
+    R, members = {}, []
+    for c in cores:
+        R[topo.chip(c), topo.die(c)] = c
+        if topo.chip(c) not in members:
+            members.append(topo.chip(c))
+    mate = {X: [Z for Z in on_chip if topo.mates(X, Z)][0] for X in on_chip}
+    nodes = members + [mate[X] for X in members if mate[X] not in members]
+    dies = sorted({topo.die(c) for c in everyone})
+    H, M = {}, {}
+    for Z in nodes:
+        for d in dies:
+            free = [c for c in on_chip[Z] if topo.die(c) == d and c not in cores]
+            H[Z, d] = [c for c in free if all(topo.may_write(c, k) for k in on_chip[mate[Z]])][0]
+            if Z in members:
+                M[Z, d] = [c for c in free if c != H[Z, d]][0]
+    plane = {Z: [X for X in members if X == Z or topo.same_plane(X, Z)] for Z in nodes}
+    ring = {Z: [Y for Y in nodes if Y == Z or topo.same_plane(Y, Z)] for Z in nodes}
+    planes = [plane[members[0]]] + [[X for X in members if X not in plane[members[0]]]]
+    rank = {c: i for i, c in enumerate(cores)}
+    slots = [rank[R[X, d]] for d in dies for p in planes for X in p]
+    calls = {c: [] for c in everyone}
+    for d in dies:
+        for X in members:
+            me = R[X, d]
+            rg = ring[X]
+            k = rg.index(X)
+            out = [H[rg[(k + s) % len(rg)], d] for s in range(1, len(rg))]
+            partner = [R[X, e] for e in dies if e != d]
+            r = rank[me]
+            calls[me].append(("cnt", slots.index(r), 1, out + [H[X, d]]))
+            calls[me].append(("blk", r, 1, out + ([H[X, d]] if mate[X] in members else []) + partner))
+        for Z in nodes:
+            h, rg = H[Z, d], ring[Z]
+            order = [d] + [e for e in dies if e != d]
+            far = [M[mate[Z], d]] if mate[Z] in members else []
+            near = [R[Z, e] for e in order] if Z in members else []
+            there = [R[mate[Z], e] for e in order] if far else []
+            src = plane[Z]
+            lo = min(slots.index(rank[R[X, d]]) for X in src)
+            calls[h].append(("cnt", lo, len(src), far + near))
+            if far:
+                calls[far[0]].append(("cnt", lo, len(src), there))
+            k = rg.index(Z)
+            for X in sorted(src, key=lambda X: (k - rg.index(X)) % len(rg)):
+                to = far + (near if X != Z else [])
+                if to:
+                    calls[h].append(("blk", rank[R[X, d]], 1, to))
+                if far:
+                    calls[far[0]].append(("blk", rank[R[X, d]], 1, there))
+    arrive = {}
+    for c in everyone:
+        for what, a, n, dsts in calls[c]:
+            name = "cin" if what == "cnt" else "b%d" % a
+            for m, ds in masks(c, dsts, topo):
+                for q in ds:
+                    arrive[q, name] = arrive.get((q, name), 0) + bin(m).count("1")
+    return {"calls": calls, "arrive": arrive, "slots": slots}
+
+
+def masks(c, dsts, topo):
+    off = [q for q in dsts if topo.chip(q) != topo.chip(c)]
+    on = [q for q in dsts if topo.chip(q) == topo.chip(c)]
+    res, m_off = [], 0
+    if off:
+        m_off = topo.mask(c, off[0])
+        res.append((m_off, off))
+    if on:
+        res.append((topo.mask(c, on[0]) & ~m_off, on))
+    return res
+
+
+def emit(g, core, T, topo, call, sent):
+    what, a, n, dsts = call
+    own = T.rank_of(core) is not None
+    if what == "cnt":
+        dst, arr = T.cnt[:, a:a + n], T.sem["cin"]
+        src = T.cinc[:, 127:128] if own else dst
+    else:
+        dst, arr = T.land[:, a * CAP:(a + 1) * CAP], T.sem["b%d" % a]
+        src = T.win[:, 0:CAP] if own else dst
+    trs = []
+    for m, ds in masks(core, dsts, topo):
+        ids = []
+        for q in ds:
+            ad = topo.addr(q)
+            ids.append(DstId(rid=ad[0], pnc=ad[1]))
+        trs.append(RemoteDMATransfer(dst_ids=ids, dma_engine_mask=m, remote_sem=arr, srcs=[src], dsts=[dst for q in ds]))
+        sent[0] += bin(m).count("1")
+    g.remote_dma_fused(trs, local_sem=T.sem.loc)
+
+
+def rank_program(g, core, T, topo):
+    if "plan" not in _cache:
+        _cache["plan"] = roles(list(T.cores), topo)
+    plan = _cache["plan"]
+    calls, arrive = plan["calls"][core], plan["arrive"]
+    if not calls:
+        return
+    sent = [0]
+    me = T.rank_of(core)
+    if me is None:
+        for call in calls:
+            name = "cin" if call[0] == "cnt" else "b%d" % call[1]
+            g.wait_ge(T.sem[name], arrive[core, name])
+            emit(g, core, T, topo, call, sent)
+        g.wait_ge(T.sem.loc, sent[0])
+        return
+
+    A = AluOpType
+    V, S, PE, sem = g.vector, g.scalar, g.tensor, T.sem
+    nv, ng = [0], [0]
+
+    def v(f, *a):
+        if nv[0]:
+            V.wait_ge(sem.vv, nv[0])
+        f(*a).then_inc(sem.vv, 1)
+        nv[0] += 1
+        return nv[0]
+
+    def gk(f, *a, **k):
+        if ng[0]:
+            g.wait_ge(sem.gk, ng[0])
+        f(*a, **k).then_inc(sem.gk, 1)
+        ng[0] += 1
+        return ng[0]
+
+    g.sync.dma_start(T.kp[:], T.keep[:]).then_inc(sem.ldk, 16)
+    S.dma_start(T.xs[:], T.x[:]).then_inc(sem.ldx, 16)
+
+    v_ones = v(V.memset, T.ones[:], 1.0)
+    v(V.memset, T.win[:, 0:CAP], 0.0)
+    v(V.memset, T.land[:, ZERO:ZERO + 16], 0.0)
+    g.wait_ge(sem.vv, v_ones)
+    gk(g.affine_select, T.half[:], T.ones[:], [[-16, 8], [0, 16]], A.is_ge, 0.0, 0, 1)
+    g_blk = gk(g.affine_select, T.blk[:], T.half[:], [[16, 8], [0, 16]], A.is_ge, 0.0, 15, -1)
+    g_tri = gk(g.affine_select, T.tri[:], T.blk[:], [[-1, 128]], A.is_ge, 0.0, 0, 1)
+    g_grid = gk(g.iota, T.tgrid[:], [[16, 128]], 512, 1, allow_small_or_imprecise_dtypes=True)
+    g_irow = gk(g.iota, T.irow[:], [[0, 8], [1, 16]], 0, 0, allow_small_or_imprecise_dtypes=True)
+
+    V.wait_ge(sem.ldk, 16)
+    v_kb = v(V.tensor_copy, T.kb[:], T.kp[:])
+    PE.wait_ge(sem.gk, g_blk)
+    PE.wait_ge(sem.vv, v_kb)
+    PE.matmul(T.psa[:, 0:128], T.blk[:], T.kb[:], True, True).then_inc(sem.pe1, 1)
+    PE.wait_ge(sem.gk, g_tri)
+    PE.matmul(T.psb[:, 0:128], T.tri[:], T.kb[:], True, True).then_inc(sem.pe2, 1)
+    v(V.tensor_scalar, T.nk[:], T.kb[:], -1.0, 1.0, A.mult, A.add)
+    V.wait_ge(sem.pe1, 1)
+    v_cnt = v(V.tensor_tensor_scan, T.cinc[:], T.ones[:], T.psa[:, 0:128], 0.0, A.mult, A.add)
+    V.wait_ge(sem.gk, g_grid)
+    v(V.tensor_tensor, T.nkt[:], T.nk[:], T.tgrid[:], A.mult)
+    V.wait_ge(sem.pe2, 1)
+    v(V.tensor_tensor, T.qf[:], T.cinc[:], T.psb[:, 0:128], A.subtract)
+    v(V.tensor_tensor, T.off[:], T.qf[:], T.nkt[:], A.max)
+    v(V.tensor_copy, T.offu[:], T.off[:])
+    V.wait_ge(sem.ldx, 16)
+    v_blk = v(V.tensor_copy, T.win[:, 0:WIN].indirect(T.offu[:, 0:128]), T.xs[:])
+    v(V.tensor_copy, T.land[:, me * CAP:(me + 1) * CAP], T.win[:, 0:CAP])
+
+    g.wait_ge(sem.vv, v_cnt)
+    emit(g, core, T, topo, calls[0], sent)
+    g.wait_ge(sem.vv, v_blk)
+    emit(g, core, T, topo, calls[1], sent)
+
+    V.wait_ge(sem.gk, g_irow)
+    imod, pcol = T.imod[:, 0:1], T.pcol[:, 0:1]
+    v(V.tensor_copy, T.pint[:, 0:1], T.tgrid[:, 0:1])
+    v(V.tensor_scalar, T.pint[:, 1:2], T.pint[:, 0:1], 15, None, A.bitwise_and)
+    v(V.tensor_copy, imod, T.pint[:, 1:2])
+    v(V.tensor_scalar, pcol, T.tgrid[:, 0:1], 512.0, None, A.subtract)
+    for k in range(4):
+        v(V.tensor_scalar, T.g16[:, 128 * k:128 * (k + 1)], T.tgrid[:], pcol, 2048.0 * k - 512.0, A.subtract, A.add)
+    v(V.tensor_scalar, T.qg[:], T.g16[:], imod, None, A.add)
+    v(V.tensor_scalar, T.ia[:], T.blk[:], 100.0, -100.0, A.mult, A.add)
+    v(V.tensor_tensor, T.imge[:], T.irow[:], T.ia[:], A.add)
+    v(V.tensor_tensor, T.imlt[:], T.irow[:], T.ia[:], A.subtract)
+    for k, r in enumerate(plan["slots"]):
+        v(V.memset, T.rr[:, k:k + 1], float(r))
+    v(V.tensor_scalar, T.mle[:], T.rr[:], imod, None, A.is_le)
+    v(V.tensor_scalar, T.meq[:], T.rr[:], imod, None, A.is_equal)
+
+    V.wait_ge(sem.cin, arrive[core, "cin"])
+    end, nn = T.pd[:, 0:1], T.nn[:, 0:1]
+    v(V.tensor_tensor, T.m1[:], T.cnt[:], T.mle[:], A.mult)
+    v(V.tensor_reduce, end, T.m1[:], AxisListType.X, A.add)
+    v(V.tensor_tensor, T.m2[:], T.cnt[:], T.meq[:], A.mult)
+    v(V.tensor_reduce, nn, T.m2[:], AxisListType.X, A.add)
+    v(V.tensor_scalar, T.pd[:, 1:2], nn, -1.0, float(CAP), A.mult, A.add)
+    v(V.tensor_copy, T.pdi[:], T.pd[:, 0:2])
+    v(V.tensor_scalar, T.bli[:, 0:2], T.pdi[:], 15, None, A.bitwise_and)
+    v(V.tensor_scalar, T.bli[:, 2:3], T.pdi[:, 1:2], 1008, None, A.bitwise_and)
+    v(V.tensor_copy, T.blf[:, 0:3], T.bli[:, 0:3])
+    b, dl, dh = T.blf[:, 0:1], T.blf[:, 1:2], T.blf[:, 2:3]
+    v(V.tensor_scalar, T.la[:], T.imge[:], b, dh, A.is_ge, A.mult)
+    v(V.tensor_scalar, T.lb[:], T.imge[:], b, dl, A.is_ge, A.mult)
+    v(V.tensor_scalar, T.lc[:], T.imlt[:], b, dh, A.is_lt, A.mult)
+    v(V.tensor_scalar, T.ld[:], T.imlt[:], b, dl, A.is_lt, A.mult)
+    v(V.tensor_scalar, T.ga[:], T.g16[:], end, -16.0, A.subtract, A.is_gt)
+    v_l = v(V.tensor_scalar, T.gb[:], T.g16[:], end, None, A.is_gt)
+    PE.wait_ge(sem.vv, v_l)
+    PE.matmul(T.psc[:], T.la[:], T.ga[:], True, False)
+    PE.matmul(T.psc[:], T.lb[:], T.ga[:], False, False)
+    PE.matmul(T.psc[:], T.lc[:], T.gb[:], False, False)
+    PE.matmul(T.psc[:], T.ld[:], T.gb[:], False, True).then_inc(sem.pe3, 1)
+    V.wait_ge(sem.pe3, 1)
+    v(V.tensor_tensor, T.srcf[:], T.psc[:], T.qg[:], A.add)
+    v(V.tensor_scalar, T.offs[:, 256:512], T.srcf[:, 256:512], float(ZERO), float(WIDE // 2), A.min, A.subtract)
+    v_list = v(V.tensor_scalar, T.offs[:, 0:256], T.srcf[:, 0:256], float(ZERO), None, A.min)
+
+    V.wait_ge(sem.vv, v_list)
+    S.wait_ge(sem.vv, v_list)
+    for part in (1, 0):
+        for r in range(part * 8, part * 8 + 8):
+            if r != me:
+                V.wait_ge(sem["b%d" % r], arrive[core, "b%d" % r])
+                S.wait_ge(sem["b%d" % r], arrive[core, "b%d" % r])
+        for k, (eng, q, w) in enumerate(PIECES):
+            if (q >= WIDE // 2) != bool(part):
+                continue
+            a = part * (WIDE // 2)
+            src = T.land[:, a:ZERO + 16].indirect(T.offs[:, q // 16:(q + w) // 16])
+            out = T.yo[:, q:q + w]
+            if eng == "v":
+                V.tensor_copy(out, src).then_inc(sem["p%d" % k], 1)
+            else:
+                S.activation(out, src, ActivationFunctionType.Copy).then_inc(sem["p%d" % k], 1)
+    for k, (eng, q, w) in enumerate(PIECES):
+        g.sync.wait_ge(sem["p%d" % k], 1)
+        g.sync.dma_start(T.y[:, q:q + w], T.yo[:, q:q + w]).then_inc(sem.ys, 16)
+    g.sync.wait_ge(sem.ys, 16 * len(PIECES))
+    g.wait_ge(sem.loc, sent[0])

@@ -13,24 +13,24 @@ def _s(cols, kind):
 
 SCRATCH = {"psa": ("psum", [128, 512], "float32"), "psb": ("psum", [128, 512], "float32"),
            "psc": ("psum", [128, 512], "float32"),
-           "kp": _s(128, "int32"), "pint": _s(2, "int32"), "pdi": _s(2, "int32"), "bli": _s(4, "int32"),
+           "kp": _s(128, "int32"), "pi": _s(4, "int32"), "bli": _s(2, "int32"),
            "offu": _s(128, "uint16"), "offs": _s(512, "uint16"),
            "xs": _s(T_COLS, "bfloat16"), "win": _s(WIN, "bfloat16"), "land": _s(WIDE + 16, "bfloat16"),
-           "yo": _s(WIDE, "bfloat16"), "ga": _s(512, "bfloat16"), "gb": _s(512, "bfloat16")}
-for _n in ("kb", "nk", "ones", "half", "blk", "tri", "irow", "ia", "imge", "imlt", "la", "lb", "lc", "ld"):
+           "yo": _s(WIDE, "bfloat16"), "cnt": _s(2 * N, "float32")}
+for _n in ("kb", "nk", "ones", "qh", "irow", "blk", "tri"):
     SCRATCH[_n] = _s(128, "bfloat16")
-for _n in ("nkt", "tgrid", "cinc", "qf", "off"):
+for _n in ("lq", "li0", "li", "ia", "imge", "imlt", "la", "lc"):
+    SCRATCH[_n] = _s(128, "float16")
+for _n in ("g16h", "oneh", "ga", "gb"):
+    SCRATCH[_n] = _s(512, "float16")
+for _n in ("qrow", "nkt", "tgrid", "cinc", "qf", "off"):
     SCRATCH[_n] = _s(128, "float32")
-for _n in ("cnt", "rr", "mle", "meq", "m1", "m2"):
-    SCRATCH[_n] = _s(N, "float32")
-for _n in ("g16", "qg", "srcf"):
-    SCRATCH[_n] = _s(512, "float32")
-for _n in ("imod", "pcol", "nn", "pd", "blf"):
+for _n in ("pf", "ee", "cs", "ed"):
     SCRATCH[_n] = _s(4, "float32")
 
 PIECES = [("v", 4096, 1024), ("s", 6144, 1024), ("v", 5120, 1024), ("s", 7168, 1024),
-          ("v", 0, 1024), ("s", 2048, 1024), ("v", 1024, 1024), ("s", 3072, 1024)]
-SEMAPHORES = (["ldk", "ldx", "vv", "gk", "pe1", "pe2", "pe3", "cin", "loc", "ys"]
+          ("v", 0, 1024), ("s", 2048, 1024), ("v", 1024, 512), ("s", 3072, 512), ("v", 1536, 512), ("s", 3584, 512)]
+SEMAPHORES = (["ldk", "ldx", "vv", "gk", "sc", "sn", "pe1", "pe2", "pe3", "cin", "loc", "ys"]
               + ["b%d" % r for r in range(N)] + ["p%d" % k for k in range(len(PIECES))])
 _cache = {}
 
@@ -63,8 +63,7 @@ def roles(cores, topo):
     calls = {c: [] for c in everyone}
     for d in dies:
         for X in members:
-            me = R[X, d]
-            rg = ring[X]
+            me, rg = R[X, d], ring[X]
             k = rg.index(X)
             out = [H[rg[(k + s) % len(rg)], d] for s in range(1, len(rg))]
             partner = [R[X, e] for e in dies if e != d]
@@ -96,7 +95,7 @@ def roles(cores, topo):
             for m, ds in masks(c, dsts, topo):
                 for q in ds:
                     arrive[q, name] = arrive.get((q, name), 0) + bin(m).count("1")
-    return {"calls": calls, "arrive": arrive, "slots": slots}
+    return {"calls": calls, "arrive": arrive}
 
 
 def masks(c, dsts, topo):
@@ -115,8 +114,8 @@ def emit(g, core, T, topo, call, sent):
     what, a, n, dsts = call
     own = T.rank_of(core) is not None
     if what == "cnt":
-        dst, arr = T.cnt[:, a:a + n], T.sem["cin"]
-        src = T.cinc[:, 127:128] if own else dst
+        dst, arr = T.cnt[:, 2 * a:2 * (a + n)], T.sem["cin"]
+        src = T.cs[:, 0:2] if own else dst
     else:
         dst, arr = T.land[:, a * CAP:(a + 1) * CAP], T.sem["b%d" % a]
         src = T.win[:, 0:CAP] if own else dst
@@ -148,9 +147,10 @@ def rank_program(g, core, T, topo):
         g.wait_ge(T.sem.loc, sent[0])
         return
 
-    A = AluOpType
+    A, F = AluOpType, ActivationFunctionType
     V, S, PE, sem = g.vector, g.scalar, g.tensor, T.sem
     nv, ng = [0], [0]
+    pnum, ph, imod = T.pf[:, 0:1], T.pf[:, 1:2], T.pf[:, 2:3]
 
     def v(f, *a):
         if nv[0]:
@@ -169,27 +169,39 @@ def rank_program(g, core, T, topo):
     g.sync.dma_start(T.kp[:], T.keep[:]).then_inc(sem.ldk, 16)
     S.dma_start(T.xs[:], T.x[:]).then_inc(sem.ldx, 16)
 
-    v_ones = v(V.memset, T.ones[:], 1.0)
-    v(V.memset, T.win[:, 0:CAP], 0.0)
-    v(V.memset, T.land[:, ZERO:ZERO + 16], 0.0)
-    g.wait_ge(sem.vv, v_ones)
-    gk(g.affine_select, T.half[:], T.ones[:], [[-16, 8], [0, 16]], A.is_ge, 0.0, 0, 1)
-    g_blk = gk(g.affine_select, T.blk[:], T.half[:], [[16, 8], [0, 16]], A.is_ge, 0.0, 15, -1)
+    cast = {"allow_small_or_imprecise_dtypes": True}
+    k = gk(g.iota, T.pi[:, 0:1], [[0, 1]], 0, 1)
+    V.wait_ge(sem.gk, k)
+    v(V.tensor_scalar, T.pi[:, 1:2], T.pi[:, 0:1], 4, None, A.arith_shift_right)
+    v(V.tensor_scalar, T.pi[:, 2:3], T.pi[:, 0:1], 15, None, A.bitwise_and)
+    v(V.tensor_copy, T.pf[:, 0:3], T.pi[:, 0:3])
+    k = gk(g.iota, T.qh[:], [[1, 8], [0, 16]], 0, 0, **cast)
+    V.wait_ge(sem.gk, k)
+    v_blk = v(V.tensor_scalar, T.blk[:], T.qh[:], ph, None, A.is_equal)
+    v(V.memset, T.ones[:], 1.0)
+    g_row = gk(g.iota, T.qrow[:], [[1, 128]], 0, 0, **cast)
+    g.wait_ge(sem.vv, v_blk)
     g_tri = gk(g.affine_select, T.tri[:], T.blk[:], [[-1, 128]], A.is_ge, 0.0, 0, 1)
-    g_grid = gk(g.iota, T.tgrid[:], [[16, 128]], 512, 1, allow_small_or_imprecise_dtypes=True)
-    g_irow = gk(g.iota, T.irow[:], [[0, 8], [1, 16]], 0, 0, allow_small_or_imprecise_dtypes=True)
+    g_irow = gk(g.iota, T.irow[:], [[0, 8], [1, 16]], 0, 0, **cast)
+    v(V.tensor_scalar, T.ee[:, 3:4], pnum, 512.0, None, A.add)
+    v(V.tensor_scalar, T.ee[:, 0:1], imod, float(me), None, A.is_ge)
+    v(V.tensor_scalar, T.ee[:, 1:2], imod, float(me), -1.0, A.is_equal, A.mult)
+    v(V.tensor_scalar, T.ee[:, 2:3], imod, float(me), float(CAP), A.is_equal, A.mult)
+    v(V.memset, T.win[:, 0:CAP], 0.0)
+    V.wait_ge(sem.gk, g_row)
+    v(V.tensor_scalar, T.tgrid[:], T.qrow[:], 16.0, T.ee[:, 3:4], A.mult, A.add)
 
     V.wait_ge(sem.ldk, 16)
     v_kb = v(V.tensor_copy, T.kb[:], T.kp[:])
-    PE.wait_ge(sem.gk, g_blk)
     PE.wait_ge(sem.vv, v_kb)
     PE.matmul(T.psa[:, 0:128], T.blk[:], T.kb[:], True, True).then_inc(sem.pe1, 1)
     PE.wait_ge(sem.gk, g_tri)
     PE.matmul(T.psb[:, 0:128], T.tri[:], T.kb[:], True, True).then_inc(sem.pe2, 1)
-    v(V.tensor_scalar, T.nk[:], T.kb[:], -1.0, 1.0, A.mult, A.add)
+    S.wait_ge(sem.vv, v_kb)
+    S.activation(T.nk[:], T.kb[:], F.Copy, bias=1.0, scale=-1.0).then_inc(sem.sn, 1)
     V.wait_ge(sem.pe1, 1)
     v_cnt = v(V.tensor_tensor_scan, T.cinc[:], T.ones[:], T.psa[:, 0:128], 0.0, A.mult, A.add)
-    V.wait_ge(sem.gk, g_grid)
+    V.wait_ge(sem.sn, 1)
     v(V.tensor_tensor, T.nkt[:], T.nk[:], T.tgrid[:], A.mult)
     V.wait_ge(sem.pe2, 1)
     v(V.tensor_tensor, T.qf[:], T.cinc[:], T.psb[:, 0:128], A.subtract)
@@ -197,57 +209,48 @@ def rank_program(g, core, T, topo):
     v(V.tensor_copy, T.offu[:], T.off[:])
     V.wait_ge(sem.ldx, 16)
     v_blk = v(V.tensor_copy, T.win[:, 0:WIN].indirect(T.offu[:, 0:128]), T.xs[:])
-    v(V.tensor_copy, T.land[:, me * CAP:(me + 1) * CAP], T.win[:, 0:CAP])
+    S.wait_ge(sem.vv, v_cnt)
+    S.activation(T.cs[:, 0:1], T.cinc[:, 127:128], F.Copy, scale=T.ee[:, 0:1]).then_inc(sem.sc, 1)
+    S.activation(T.cs[:, 1:2], T.cinc[:, 127:128], F.Identity, bias=T.ee[:, 2:3], scale=T.ee[:, 1:2]).then_inc(sem.sc, 1)
 
-    g.wait_ge(sem.vv, v_cnt)
+    g.wait_ge(sem.sc, 2)
     emit(g, core, T, topo, calls[0], sent)
     g.wait_ge(sem.vv, v_blk)
     emit(g, core, T, topo, calls[1], sent)
 
     V.wait_ge(sem.gk, g_irow)
-    imod, pcol = T.imod[:, 0:1], T.pcol[:, 0:1]
-    v(V.tensor_copy, T.pint[:, 0:1], T.tgrid[:, 0:1])
-    v(V.tensor_scalar, T.pint[:, 1:2], T.pint[:, 0:1], 15, None, A.bitwise_and)
-    v(V.tensor_copy, imod, T.pint[:, 1:2])
-    v(V.tensor_scalar, pcol, T.tgrid[:, 0:1], 512.0, None, A.subtract)
     for k in range(4):
-        v(V.tensor_scalar, T.g16[:, 128 * k:128 * (k + 1)], T.tgrid[:], pcol, 2048.0 * k - 512.0, A.subtract, A.add)
-    v(V.tensor_scalar, T.qg[:], T.g16[:], imod, None, A.add)
+        v(V.tensor_scalar, T.g16h[:, 128 * k:128 * (k + 1)], T.qrow[:], 16.0, 2048.0 * k, A.mult, A.add)
+    v(V.tensor_scalar, T.oneh[:], T.g16h[:], 0.0, 1.0, A.mult, A.add)
+    v(V.tensor_scalar, T.lq[:], T.blk[:], 0.0625, None, A.mult)
+    v(V.tensor_tensor, T.li0[:], T.blk[:], T.irow[:], A.mult)
+    v_q = v(V.tensor_scalar, T.li[:], T.li0[:], 0.0625, None, A.mult)
     v(V.tensor_scalar, T.ia[:], T.blk[:], 100.0, -100.0, A.mult, A.add)
     v(V.tensor_tensor, T.imge[:], T.irow[:], T.ia[:], A.add)
     v(V.tensor_tensor, T.imlt[:], T.irow[:], T.ia[:], A.subtract)
-    for k, r in enumerate(plan["slots"]):
-        v(V.memset, T.rr[:, k:k + 1], float(r))
-    v(V.tensor_scalar, T.mle[:], T.rr[:], imod, None, A.is_le)
-    v(V.tensor_scalar, T.meq[:], T.rr[:], imod, None, A.is_equal)
+    v(V.memset, T.land[:, ZERO:ZERO + 16], 0.0)
+    v(V.tensor_copy, T.land[:, me * CAP:(me + 1) * CAP], T.win[:, 0:CAP])
+    PE.wait_ge(sem.vv, v_q)
+    PE.matmul(T.psc[:], T.lq[:], T.g16h[:], True, False)
+    PE.matmul(T.psc[:], T.li[:], T.oneh[:], False, False)
 
     V.wait_ge(sem.cin, arrive[core, "cin"])
-    end, nn = T.pd[:, 0:1], T.nn[:, 0:1]
-    v(V.tensor_tensor, T.m1[:], T.cnt[:], T.mle[:], A.mult)
-    v(V.tensor_reduce, end, T.m1[:], AxisListType.X, A.add)
-    v(V.tensor_tensor, T.m2[:], T.cnt[:], T.meq[:], A.mult)
-    v(V.tensor_reduce, nn, T.m2[:], AxisListType.X, A.add)
-    v(V.tensor_scalar, T.pd[:, 1:2], nn, -1.0, float(CAP), A.mult, A.add)
-    v(V.tensor_copy, T.pdi[:], T.pd[:, 0:2])
-    v(V.tensor_scalar, T.bli[:, 0:2], T.pdi[:], 15, None, A.bitwise_and)
-    v(V.tensor_scalar, T.bli[:, 2:3], T.pdi[:, 1:2], 1008, None, A.bitwise_and)
-    v(V.tensor_copy, T.blf[:, 0:3], T.bli[:, 0:3])
-    b, dl, dh = T.blf[:, 0:1], T.blf[:, 1:2], T.blf[:, 2:3]
-    v(V.tensor_scalar, T.la[:], T.imge[:], b, dh, A.is_ge, A.mult)
-    v(V.tensor_scalar, T.lb[:], T.imge[:], b, dl, A.is_ge, A.mult)
-    v(V.tensor_scalar, T.lc[:], T.imlt[:], b, dh, A.is_lt, A.mult)
-    v(V.tensor_scalar, T.ld[:], T.imlt[:], b, dl, A.is_lt, A.mult)
-    v(V.tensor_scalar, T.ga[:], T.g16[:], end, -16.0, A.subtract, A.is_gt)
-    v_l = v(V.tensor_scalar, T.gb[:], T.g16[:], end, None, A.is_gt)
-    PE.wait_ge(sem.vv, v_l)
-    PE.matmul(T.psc[:], T.la[:], T.ga[:], True, False)
-    PE.matmul(T.psc[:], T.lb[:], T.ga[:], False, False)
-    PE.matmul(T.psc[:], T.lc[:], T.gb[:], False, False)
-    PE.matmul(T.psc[:], T.ld[:], T.gb[:], False, True).then_inc(sem.pe3, 1)
+    end, d, b = T.ed[:, 0:1], T.ed[:, 1:2], T.ed[:, 2:3]
+    v(V.tensor_reduce, end, T.cnt[:, 0:2 * N:2], AxisListType.X, A.add)
+    v(V.tensor_scalar, T.bli[:, 0:1], end, 0.0625, -0.46875, A.mult, A.add)
+    v(V.tensor_scalar, b, T.bli[:, 0:1], -16.0, end, A.mult, A.add)
+    v(V.tensor_reduce, d, T.cnt[:, 1:2 * N:2], AxisListType.X, A.add)
+    v(V.tensor_scalar, T.la[:], T.imge[:], b, d, A.is_ge, A.mult)
+    v_a = v(V.tensor_scalar, T.ga[:], T.g16h[:], end, -16.0, A.subtract, A.is_gt)
+    v(V.tensor_scalar, T.lc[:], T.imlt[:], b, d, A.is_lt, A.mult)
+    v_b = v(V.tensor_scalar, T.gb[:], T.g16h[:], end, None, A.is_gt)
+    PE.wait_ge(sem.vv, v_a)
+    PE.matmul(T.psc[:], T.la[:], T.ga[:], False, False)
+    PE.wait_ge(sem.vv, v_b)
+    PE.matmul(T.psc[:], T.lc[:], T.gb[:], False, True).then_inc(sem.pe3, 1)
     V.wait_ge(sem.pe3, 1)
-    v(V.tensor_tensor, T.srcf[:], T.psc[:], T.qg[:], A.add)
-    v(V.tensor_scalar, T.offs[:, 256:512], T.srcf[:, 256:512], float(ZERO), float(WIDE // 2), A.min, A.subtract)
-    v_list = v(V.tensor_scalar, T.offs[:, 0:256], T.srcf[:, 0:256], float(ZERO), None, A.min)
+    v(V.tensor_scalar, T.offs[:, 256:512], T.psc[:, 256:512], float(ZERO), float(WIDE // 2), A.min, A.subtract)
+    v_list = v(V.tensor_scalar, T.offs[:, 0:256], T.psc[:, 0:256], float(ZERO), None, A.min)
 
     V.wait_ge(sem.vv, v_list)
     S.wait_ge(sem.vv, v_list)
@@ -265,7 +268,7 @@ def rank_program(g, core, T, topo):
             if eng == "v":
                 V.tensor_copy(out, src).then_inc(sem["p%d" % k], 1)
             else:
-                S.activation(out, src, ActivationFunctionType.Copy).then_inc(sem["p%d" % k], 1)
+                S.activation(out, src, F.Copy).then_inc(sem["p%d" % k], 1)
     for k, (eng, q, w) in enumerate(PIECES):
         g.sync.wait_ge(sem["p%d" % k], 1)
         g.sync.dma_start(T.y[:, q:q + w], T.yo[:, q:q + w]).then_inc(sem.ys, 16)

from concourse.bass import DstId, RemoteDMATransfer
from concourse.mybir import AluOpType, AxisListType, ActivationFunctionType

N, CAP, T_COLS = 16, 512, 2048
WIDE = N * CAP
ZERO = WIDE
WIN = 2688


def _s(cols, kind):
    return ("sbuf", [128, cols], kind)


SCRATCH = {"psa": ("psum", [128, 512], "float32"), "psb": ("psum", [128, 512], "float32"),
           "psc": ("psum", [128, 512], "float32"),
           "kp": _s(128, "int32"), "pi": _s(4, "int32"), "bli": _s(2, "int32"),
           "offu": _s(128, "uint16"), "offs": _s(512, "uint16"),
           "xs": _s(T_COLS, "bfloat16"), "win": _s(WIN, "bfloat16"), "land": _s(WIDE + 16, "bfloat16"),
           "yo": _s(WIDE, "bfloat16"), "cnt": _s(2 * N, "float32")}
for _n in ("kb", "nk", "ones", "qh", "irow", "blk", "tri"):
    SCRATCH[_n] = _s(128, "bfloat16")
for _n in ("lq", "li0", "li", "ia", "imge", "imlt", "la", "lc"):
    SCRATCH[_n] = _s(128, "float16")
for _n in ("g16h", "oneh", "ga", "gb"):
    SCRATCH[_n] = _s(512, "float16")
for _n in ("qrow", "nkt", "tgrid", "cinc", "qf", "off"):
    SCRATCH[_n] = _s(128, "float32")
for _n in ("pf", "ee", "cs", "ed"):
    SCRATCH[_n] = _s(4, "float32")

PIECES = [("v", 4096, 1024), ("s", 6144, 1024), ("v", 5120, 1024), ("s", 7168, 1024),
          ("v", 0, 1024), ("s", 2048, 1024), ("v", 1024, 512), ("s", 3072, 512), ("v", 1536, 512), ("s", 3584, 512)]
SEMAPHORES = (["ldk", "ldx", "vv", "gk", "sc", "sn", "pe1", "pe2", "pe3", "cin", "loc", "ys"]
              + ["b%d" % r for r in range(N)] + ["p%d" % k for k in range(len(PIECES))])
_cache = {}


def roles(cores, topo):
    everyone = range(128)
    on_chip = {}
    for c in everyone:
        on_chip.setdefault(topo.chip(c), []).append(c)
    R, members = {}, []
    for c in cores:
        R[topo.chip(c), topo.die(c)] = c
        if topo.chip(c) not in members:
            members.append(topo.chip(c))
    mate = {X: [Z for Z in on_chip if topo.mates(X, Z)][0] for X in on_chip}
    nodes = members + [mate[X] for X in members if mate[X] not in members]
    dies = sorted({topo.die(c) for c in everyone})
    H, M = {}, {}
    for Z in nodes:
        for d in dies:
            free = [c for c in on_chip[Z] if topo.die(c) == d and c not in cores]
            H[Z, d] = [c for c in free if all(topo.may_write(c, k) for k in on_chip[mate[Z]])][0]
            if Z in members:
                M[Z, d] = [c for c in free if c != H[Z, d]][0]
    plane = {Z: [X for X in members if X == Z or topo.same_plane(X, Z)] for Z in nodes}
    ring = {Z: [Y for Y in nodes if Y == Z or topo.same_plane(Y, Z)] for Z in nodes}
    planes = [plane[members[0]]] + [[X for X in members if X not in plane[members[0]]]]
    rank = {c: i for i, c in enumerate(cores)}
    slots = [rank[R[X, d]] for d in dies for p in planes for X in p]
    calls = {c: [] for c in everyone}
    for d in dies:
        for X in members:
            me, rg = R[X, d], ring[X]
            k = rg.index(X)
            out = [H[rg[(k + s) % len(rg)], d] for s in range(1, len(rg))]
            partner = [R[X, e] for e in dies if e != d]
            r = rank[me]
            calls[me].append(("cnt", slots.index(r), 1, out + [H[X, d]]))
            calls[me].append(("blk", r, 1, out + ([H[X, d]] if mate[X] in members else []) + partner))
        for Z in nodes:
            h, rg = H[Z, d], ring[Z]
            order = [d] + [e for e in dies if e != d]
            far = [M[mate[Z], d]] if mate[Z] in members else []
            near = [R[Z, e] for e in order] if Z in members else []
            there = [R[mate[Z], e] for e in order] if far else []
            src = plane[Z]
            lo = min(slots.index(rank[R[X, d]]) for X in src)
            calls[h].append(("cnt", lo, len(src), far + near))
            if far:
                calls[far[0]].append(("cnt", lo, len(src), there))
            k = rg.index(Z)
            for X in sorted(src, key=lambda X: (k - rg.index(X)) % len(rg)):
                to = far + (near if X != Z else [])
                if to:
                    calls[h].append(("blk", rank[R[X, d]], 1, to))
                if far:
                    calls[far[0]].append(("blk", rank[R[X, d]], 1, there))
    arrive = {}
    for c in everyone:
        for what, a, n, dsts in calls[c]:
            name = "cin" if what == "cnt" else "b%d" % a
            for m, ds in masks(c, dsts, topo):
                for q in ds:
                    arrive[q, name] = arrive.get((q, name), 0) + bin(m).count("1")
    return {"calls": calls, "arrive": arrive}


def masks(c, dsts, topo):
    off = [q for q in dsts if topo.chip(q) != topo.chip(c)]
    on = [q for q in dsts if topo.chip(q) == topo.chip(c)]
    res, m_off = [], 0
    if off:
        m_off = topo.mask(c, off[0])
        res.append((m_off, off))
    if on:
        res.append((topo.mask(c, on[0]) & ~m_off, on))
    return res


def emit(g, core, T, topo, call, sent):
    what, a, n, dsts = call
    own = T.rank_of(core) is not None
    if what == "cnt":
        dst, arr = T.cnt[:, 2 * a:2 * (a + n)], T.sem["cin"]
        src = T.cs[:, 0:2] if own else dst
    else:
        dst, arr = T.land[:, a * CAP:(a + 1) * CAP], T.sem["b%d" % a]
        src = T.win[:, 0:CAP] if own else dst
    trs = []
    for m, ds in masks(core, dsts, topo):
        ids = []
        for q in ds:
            ad = topo.addr(q)
            ids.append(DstId(rid=ad[0], pnc=ad[1]))
        trs.append(RemoteDMATransfer(dst_ids=ids, dma_engine_mask=m, remote_sem=arr, srcs=[src], dsts=[dst for q in ds]))
        sent[0] += bin(m).count("1")
    g.remote_dma_fused(trs, local_sem=T.sem.loc)


def rank_program(g, core, T, topo):
    if "plan" not in _cache:
        _cache["plan"] = roles(list(T.cores), topo)
    plan = _cache["plan"]
    calls, arrive = plan["calls"][core], plan["arrive"]
    if not calls:
        return
    sent = [0]
    me = T.rank_of(core)
    if me is None:
        for call in calls:
            name = "cin" if call[0] == "cnt" else "b%d" % call[1]
            g.wait_ge(T.sem[name], arrive[core, name])
            emit(g, core, T, topo, call, sent)
        g.wait_ge(T.sem.loc, sent[0])
        return

    A, F = AluOpType, ActivationFunctionType
    V, S, PE, sem = g.vector, g.scalar, g.tensor, T.sem
    nv, ng = [0], [0]
    pnum, ph, imod = T.pf[:, 0:1], T.pf[:, 1:2], T.pf[:, 2:3]

    def v(f, *a):
        if nv[0]:
            V.wait_ge(sem.vv, nv[0])
        f(*a).then_inc(sem.vv, 1)
        nv[0] += 1
        return nv[0]

    def gk(f, *a, **k):
        if ng[0]:
            g.wait_ge(sem.gk, ng[0])
        f(*a, **k).then_inc(sem.gk, 1)
        ng[0] += 1
        return ng[0]

    g.sync.dma_start(T.kp[:], T.keep[:]).then_inc(sem.ldk, 16)
    S.dma_start(T.xs[:], T.x[:]).then_inc(sem.ldx, 16)

    cast = {"allow_small_or_imprecise_dtypes": True}
    k = gk(g.iota, T.pi[:, 0:1], [[0, 1]], 0, 1)
    V.wait_ge(sem.gk, k)
    v(V.tensor_scalar, T.pi[:, 1:2], T.pi[:, 0:1], 4, None, A.arith_shift_right)
    v(V.tensor_scalar, T.pi[:, 2:3], T.pi[:, 0:1], 15, None, A.bitwise_and)
    v(V.tensor_copy, T.pf[:, 0:3], T.pi[:, 0:3])
    k = gk(g.iota, T.qh[:], [[1, 8], [0, 16]], 0, 0, **cast)
    V.wait_ge(sem.gk, k)
    v_blk = v(V.tensor_scalar, T.blk[:], T.qh[:], ph, None, A.is_equal)
    v(V.memset, T.ones[:], 1.0)
    g_row = gk(g.iota, T.qrow[:], [[1, 128]], 0, 0, **cast)
    g.wait_ge(sem.vv, v_blk)
    g_tri = gk(g.affine_select, T.tri[:], T.blk[:], [[-1, 128]], A.is_ge, 0.0, 0, 1)
    g_irow = gk(g.iota, T.irow[:], [[0, 8], [1, 16]], 0, 0, **cast)
    v(V.tensor_scalar, T.ee[:, 3:4], pnum, 512.0, None, A.add)
    v(V.tensor_scalar, T.ee[:, 0:1], imod, float(me), None, A.is_ge)
    v(V.tensor_scalar, T.ee[:, 1:2], imod, float(me), -1.0, A.is_equal, A.mult)
    v(V.tensor_scalar, T.ee[:, 2:3], imod, float(me), float(CAP), A.is_equal, A.mult)
    v(V.memset, T.win[:, 0:CAP], 0.0)
    V.wait_ge(sem.gk, g_row)
    v(V.tensor_scalar, T.tgrid[:], T.qrow[:], 16.0, T.ee[:, 3:4], A.mult, A.add)

    V.wait_ge(sem.ldk, 16)
    v_kb = v(V.tensor_copy, T.kb[:], T.kp[:])
    PE.wait_ge(sem.vv, v_kb)
    PE.matmul(T.psa[:, 0:128], T.blk[:], T.kb[:], True, True).then_inc(sem.pe1, 1)
    PE.wait_ge(sem.gk, g_tri)
    PE.matmul(T.psb[:, 0:128], T.tri[:], T.kb[:], True, True).then_inc(sem.pe2, 1)
    S.wait_ge(sem.vv, v_kb)
    S.activation(T.nk[:], T.kb[:], F.Copy, bias=1.0, scale=-1.0).then_inc(sem.sn, 1)
    V.wait_ge(sem.pe1, 1)
    v_cnt = v(V.tensor_tensor_scan, T.cinc[:], T.ones[:], T.psa[:, 0:128], 0.0, A.mult, A.add)
    V.wait_ge(sem.sn, 1)
    v(V.tensor_tensor, T.nkt[:], T.nk[:], T.tgrid[:], A.mult)
    V.wait_ge(sem.pe2, 1)
    v(V.tensor_tensor, T.qf[:], T.cinc[:], T.psb[:, 0:128], A.subtract)
    v(V.tensor_tensor, T.off[:], T.qf[:], T.nkt[:], A.max)
    v(V.tensor_copy, T.offu[:], T.off[:])
    V.wait_ge(sem.ldx, 16)
    v_blk = v(V.tensor_copy, T.win[:, 0:WIN].indirect(T.offu[:, 0:128]), T.xs[:])
    S.wait_ge(sem.vv, v_cnt)
    S.activation(T.cs[:, 0:1], T.cinc[:, 127:128], F.Copy, scale=T.ee[:, 0:1]).then_inc(sem.sc, 1)
    S.activation(T.cs[:, 1:2], T.cinc[:, 127:128], F.Identity, bias=T.ee[:, 2:3], scale=T.ee[:, 1:2]).then_inc(sem.sc, 1)

    g.wait_ge(sem.sc, 2)
    emit(g, core, T, topo, calls[0], sent)
    g.wait_ge(sem.vv, v_blk)
    emit(g, core, T, topo, calls[1], sent)

    V.wait_ge(sem.gk, g_irow)
    for k in range(4):
        v(V.tensor_scalar, T.g16h[:, 128 * k:128 * (k + 1)], T.qrow[:], 16.0, 2048.0 * k, A.mult, A.add)
    v(V.tensor_scalar, T.oneh[:], T.g16h[:], 0.0, 1.0, A.mult, A.add)
    v(V.tensor_scalar, T.lq[:], T.blk[:], 0.0625, None, A.mult)
    v(V.tensor_tensor, T.li0[:], T.blk[:], T.irow[:], A.mult)
    v_q = v(V.tensor_scalar, T.li[:], T.li0[:], 0.0625, None, A.mult)
    v(V.tensor_scalar, T.ia[:], T.blk[:], 100.0, -100.0, A.mult, A.add)
    v(V.tensor_tensor, T.imge[:], T.irow[:], T.ia[:], A.add)
    v(V.tensor_tensor, T.imlt[:], T.irow[:], T.ia[:], A.subtract)
    v(V.memset, T.land[:, ZERO:ZERO + 16], 0.0)
    v(V.tensor_copy, T.land[:, me * CAP:(me + 1) * CAP], T.win[:, 0:CAP])
    PE.wait_ge(sem.vv, v_q)
    PE.matmul(T.psc[:], T.lq[:], T.g16h[:], True, False)
    PE.matmul(T.psc[:], T.li[:], T.oneh[:], False, False)

    V.wait_ge(sem.cin, arrive[core, "cin"])
    end, d, b = T.ed[:, 0:1], T.ed[:, 1:2], T.ed[:, 2:3]
    v(V.tensor_reduce, end, T.cnt[:, 0:2 * N:2], AxisListType.X, A.add)
    v(V.tensor_scalar, T.bli[:, 0:1], end, 0.0625, -0.46875, A.mult, A.add)
    v(V.tensor_scalar, b, T.bli[:, 0:1], -16.0, end, A.mult, A.add)
    v(V.tensor_reduce, d, T.cnt[:, 1:2 * N:2], AxisListType.X, A.add)
    v(V.tensor_scalar, T.la[:], T.imge[:], b, d, A.is_ge, A.mult)
    v_a = v(V.tensor_scalar, T.ga[:], T.g16h[:], end, -16.0, A.subtract, A.is_gt)
    v(V.tensor_scalar, T.lc[:], T.imlt[:], b, d, A.is_lt, A.mult)
    v_b = v(V.tensor_scalar, T.gb[:], T.g16h[:], end, None, A.is_gt)
    PE.wait_ge(sem.vv, v_a)
    PE.matmul(T.psc[:], T.la[:], T.ga[:], False, False)
    PE.wait_ge(sem.vv, v_b)
    PE.matmul(T.psc[:], T.lc[:], T.gb[:], False, True).then_inc(sem.pe3, 1)
    V.wait_ge(sem.pe3, 1)
    v(V.tensor_scalar, T.offs[:, 256:512], T.psc[:, 256:512], float(ZERO), float(WIDE // 2), A.min, A.subtract)
    v_list = v(V.tensor_scalar, T.offs[:, 0:256], T.psc[:, 0:256], float(ZERO), None, A.min)

    V.wait_ge(sem.vv, v_list)
    S.wait_ge(sem.vv, v_list)
    for part in (1, 0):
        for r in range(part * 8, part * 8 + 8):
            if r != me:
                V.wait_ge(sem["b%d" % r], arrive[core, "b%d" % r])
                S.wait_ge(sem["b%d" % r], arrive[core, "b%d" % r])
        for k, (eng, q, w) in enumerate(PIECES):
            if (q >= WIDE // 2) != bool(part):
                continue
            a = part * (WIDE // 2)
            src = T.land[:, a:ZERO + 16].indirect(T.offs[:, q // 16:(q + w) // 16])
            out = T.yo[:, q:q + w]
            if eng == "v":
                V.tensor_copy(out, src).then_inc(sem["p%d" % k], 1)
            else:
                S.activation(out, src, F.Copy).then_inc(sem["p%d" % k], 1)
    for k, (eng, q, w) in enumerate(PIECES):
        g.sync.wait_ge(sem["p%d" % k], 1)
        g.sync.dma_start(T.y[:, q:q + w], T.yo[:, q:q + w]).then_inc(sem.ys, 16)
    g.sync.wait_ge(sem.ys, 16 * len(PIECES))
    g.wait_ge(sem.loc, sent[0])
